import numpy as np
import ml_dtypes


def mxq(x, axis, fmt="e4m3"):
    dtype, down = {"e4m3": (ml_dtypes.float8_e4m3fn, 7), "e5m2": (ml_dtypes.float8_e5m2, 14)}[fmt]
    v = np.moveaxis(np.asarray(x, np.float32).astype(ml_dtypes.bfloat16).astype(np.float64), axis, -1)
    blocks = v.reshape(v.shape[:-1] + (-1, 32))
    amax = np.abs(blocks).max(-1, keepdims=True)
    byte = np.maximum(np.where(amax > 0, np.frexp(amax)[1] - 1 + 127, 0) - down, 1)
    scale = np.exp2(byte - 127.0)
    codes = (blocks / scale).astype(np.float32).astype(dtype).astype(np.float64)
    return np.moveaxis((codes * scale).reshape(v.shape), -1, axis)


WIDE = False


def mx_kscale(k):
    if not WIDE:
        return np.ones(k)
    levels = np.array([10, -10, 5, -5, 0])
    if k % 512:
        return np.exp2(np.random.permutation(np.resize(levels, k // 32))).repeat(32)
    a = np.empty((k // 512, 16))
    for p in range(k // 512):
        a[p, :8] = np.random.permutation(np.resize(levels, 8))
        for g in range(8):
            far = levels[np.abs(levels - a[p, g]) >= 10]
            a[p, g + 8] = far[np.random.randint(len(far))]
    return np.exp2(a.ravel()).repeat(32)


def f64(x):
    return np.asarray(x).astype(np.float64)


def striped(idx):
    return np.tile(np.asarray(idx).reshape(-1, 16).T, (8, 1)).astype(np.uint16)


def unstriped(offs):
    return offs[:16].T.reshape(-1).astype(np.int64)


E2M1 = np.array([0.0, 0.5, 1.0, 1.5, 2.0, 3.0, 4.0, 6.0, -0.0, -0.5, -1.0, -1.5, -2.0, -3.0, -4.0, -6.0])


def pack_weight(w, fmt):
    k, n = w.shape
    w = f64(np.asarray(w, np.float32).astype(ml_dtypes.bfloat16)).reshape(k // 32, 32, n)
    amax = np.abs(w).max(1)
    if fmt == "e4m3":
        byte = np.frexp(amax)[1] - 1 + 127 - 7
    else:
        mant, ex = np.frexp(amax / 6.0)
        byte = np.where(mant > 0.5, ex, ex - 1) + 127
    byte = np.clip(np.where(amax > 0, byte, 1), 1, 254)
    scaled = (w * np.exp2(127.0 - byte)[:, None, :]).reshape(k, n).astype(np.float32)
    by_word = np.ascontiguousarray(scaled.reshape(k // 512, 128, 4, n).transpose(0, 1, 3, 2))
    if fmt == "e4m3":
        words = by_word.astype(ml_dtypes.float8_e4m3fn).view(np.uint8)
    else:
        c = by_word.astype(ml_dtypes.float4_e2m1fn).view(np.uint8) & 0xF
        words = (c[..., 0::2] | (c[..., 1::2] << 4)).reshape(k // 512, 128, 2 * n)
    return np.ascontiguousarray(words), np.ascontiguousarray(byte.astype(np.uint8).reshape(k // 512, 16, n))


def unpack_weight(words, scales, fmt):
    g, _, n = scales.shape
    words = np.ascontiguousarray(words).reshape(g, 128, n, -1)
    if fmt == "e4m3":
        vals = words.view(ml_dtypes.float8_e4m3fn).astype(np.float64)
    else:
        nib = np.empty((g, 128, n, 4), np.uint8)
        nib[..., 0::2] = words & 0xF
        nib[..., 1::2] = words >> 4
        vals = E2M1[nib]
    vals = vals * np.repeat(np.exp2(scales.astype(np.float64) - 127.0), 8, axis=1)[..., None]
    return vals.transpose(0, 1, 3, 2).reshape(g * 512, n)


def bf(x):
    return np.asarray(x, np.float32).astype(ml_dtypes.bfloat16)


def planes(Y):
    r, m = Y.shape
    b = f64(bf(Y)).reshape(r // 32, 32, m)
    amax = np.abs(b).max(1)
    byte = np.clip(np.where(amax > 0, np.frexp(amax)[1] - 1 + 127 - 7, 1), 1, 254)
    codes = (b * np.exp2(127.0 - byte)[:, None, :]).reshape(r, m).astype(np.float32).astype(ml_dtypes.float8_e4m3fn).view(np.uint8)
    words = codes.reshape(r // 512, 128, 4, m).transpose(0, 1, 3, 2)
    return np.ascontiguousarray(words), np.ascontiguousarray(byte.astype(np.uint8).reshape(r // 512, 16, m))


K, T, J, R, N = 512, 2048, 512, 512, 512


def setup_inputs():
    n = np.random.standard_normal
    idx = np.random.permutation(T)[:J]
    fk = mx_kscale(K)
    fr = mx_kscale(R)
    xtp = pack_weight(n((K, T)) / fk[:, None], "e2m1")
    wap = pack_weight(n((K, R)) * 1 / np.sqrt(K) * fk[:, None] * fr, "e4m3")
    wbp = pack_weight(n((R, N)) * 1 / np.sqrt(R) / fr[:, None], "e2m1")
    return {
        "xt_words": xtp[0],
        "xt_scales": xtp[1],
        "wa_words": wap[0],
        "wa_scales": wap[1],
        "dc": (np.random.uniform(0.3, 0.9, (R, 1))).astype(np.float32),
        "wb_words": wbp[0],
        "wb_scales": wbp[1],
        "rw": (np.random.uniform(0.5, 2.0, (1, J))).astype(np.float32),
        "offs": striped(idx),
    }


def reference(xt_words, xt_scales, wa_words, wa_scales, dc, wb_words, wb_scales, rw, offs):
    idx = unstriped(offs)
    xtu = unpack_weight(xt_words, xt_scales, "e2m1")
    wau = unpack_weight(wa_words, wa_scales, "e4m3")
    wbu = unpack_weight(wb_words, wb_scales, "e2m1")
    xtidxg = xtu[:, idx]
    a = wau.T @ xtidxg
    h1 = np.maximum(a, 0.0)
    hp = np.pad(h1, ((0, 0), (1, 0)))[:, :J]
    hid = h1 + f64(dc) * hp
    hidq = mxq(hid, 0, "e4m3")
    p = wbu.T @ hidq
    y = p * f64(rw)
    words, scales = planes(y)
    return y, words, scales

@@ -1,0 +1,222 @@
+from contextlib import ExitStack
+
+import concourse.mybir as mybir
+
+F32 = mybir.dt.float32
+BF16 = mybir.dt.bfloat16
+I32 = mybir.dt.int32
+U32 = mybir.dt.uint32
+U16 = mybir.dt.uint16
+U8 = mybir.dt.uint8
+FP8X4 = mybir.dt.float8_e4m3fn_x4
+FP4X4 = mybir.dt.float4_e2m1fn_x4
+ALU = mybir.AluOpType
+ACT = mybir.ActivationFunctionType
+
+P = 128
+T = 2048
+J = 512
+W = 512
+PACK = 4
+CH = 128
+NCH = J // CH
+HALF = 256
+PAD = 4
+FLOPS = 2 * 2 * 512 * 512 * 512
+
+
+def tile_list_hidden_with_previous_pl_kernel(
+    tc, xt_words, xt_scales, wa_words, wa_scales, dc, wb_words, wb_scales, rw, offs, out_0, out_1, out_2
+):
+    nc = tc.nc
+    with ExitStack() as ctx:
+        keep = ctx.enter_context(tc.tile_pool(name="keep", bufs=1))
+        psum = ctx.enter_context(tc.psum_pool(name="psum", bufs=1))
+
+        offsets = keep.tile([P, J // 16], U16, name="offsets")
+        xt_win = keep.tile([P, T], U16, name="xt_win", align_bytes=64)
+        xs_win = keep.tile([P, T], U8, name="xs_win", align_bytes=64)
+        wa_raw = keep.tile([P, W], I32, name="wa_raw", align_bytes=64)
+        was_raw = keep.tile([P, W], U8, name="was_raw", align_bytes=64)
+        wb_raw = keep.tile([P, W], U16, name="wb_raw", align_bytes=64)
+        wbs_raw = keep.tile([P, W], U8, name="wbs_raw", align_bytes=64)
+        wa_d = keep.tile([P, W], I32, name="wa_d", align_bytes=64)
+        was_d = keep.tile([P, W], U8, name="was_d", align_bytes=64)
+        wb_d = keep.tile([P, W], U16, name="wb_d", align_bytes=64)
+        wbs_d = keep.tile([P, W], U8, name="wbs_d", align_bytes=64)
+        dc_sb = keep.tile([P, PACK], F32, name="dc_sb")
+        rw_sb = keep.tile([P, J], F32, name="rw_sb")
+        xg = [keep.tile([P, HALF], U16, name="xg%d" % i, align_bytes=64) for i in range(2)]
+        sg = [keep.tile([P, HALF], U8, name="sg%d" % i, align_bytes=64) for i in range(2)]
+        h1 = keep.tile([P, PACK, J + 2 * PAD], F32, name="h1", align_bytes=64)
+        warm = keep.tile([P, 1], F32, name="warm")
+        y_codes = keep.tile([P, J], U32, name="y_codes", align_bytes=64)
+        y_scales = keep.tile([P, J], U8, name="y_scales", align_bytes=64)
+
+        def load_scale_rows(queue, tile, src, q):
+            queue.dma_start(
+                out=tile[32 * q : 32 * q + 4, :].bitcast(I32), in_=src[0, 4 * q : 4 * q + 4, :].bitcast(I32)
+            )
+
+        def deal(dst, src):
+            nc.vector.tensor_copy(
+                out=dst[:].rearrange("p (t q) -> p t q", t=PACK), in_=src[:].rearrange("p (q t) -> p t q", t=PACK)
+            )
+
+        nc.vector.memset(xs_win[:].bitcast(I32), 0)
+        nc.vector.memset(was_raw[:].bitcast(I32), 0)
+        nc.vector.memset(wbs_raw[:].bitcast(I32), 0)
+        nc.vector.memset(h1[:, :, 0:PAD], 0.0)
+
+        nc.sync.dma_start(offsets[:], offs)
+        for q in range(4):
+            load_scale_rows(nc.scalar, xs_win, xt_scales, q)
+        nc.sync.dma_start(out=xt_win[:].bitcast(I32), in_=xt_words[0].bitcast(I32))
+        nc.sync.dma_start(out=wa_raw[:], in_=wa_words[0].rearrange("p n t -> p (n t)").bitcast(I32))
+        for q in range(4):
+            load_scale_rows(nc.sync, was_raw, wa_scales, q)
+        nc.gpsimd.dma_start(out=dc_sb[:], in_=dc.rearrange("(p t) o -> p (t o)", t=PACK))
+        nc.sync.dma_start(out=wb_raw[:].bitcast(I32), in_=wb_words[0].bitcast(I32))
+        for q in range(4):
+            load_scale_rows(nc.sync, wbs_raw, wb_scales, q)
+        nc.gpsimd.dma_start(out=rw_sb[:], in_=rw[0].partition_broadcast(P))
+        nc.scalar.activation(out=warm[:], in_=h1[:, 0, 0:1], func=ACT.Relu)
+
+        def gather(i):
+            lst = offsets[:, i * (HALF // 16) : (i + 1) * (HALF // 16)]
+            nc.vector.tensor_copy(sg[i][:], xs_win[:].indirect(lst))
+            nc.vector.tensor_copy(xg[i][:], xt_win[:].indirect(lst))
+
+        a_bank = [psum.tile([P, PACK, CH], F32, name="a%d" % c) for c in range(NCH)]
+        p_bank = [psum.tile([P, PACK, CH], F32, name="p%d" % c) for c in range(NCH)]
+        hid_rows = [keep.tile([P, PACK, CH], BF16, name="hr%d" % c, align_bytes=64) for c in range(NCH)]
+        hid_il = [keep.tile([P, CH, PACK], BF16, name="hi%d" % c, align_bytes=64) for c in range(NCH)]
+        hid_codes = [keep.tile([P, CH], U32, name="hc%d" % c, align_bytes=64) for c in range(NCH)]
+        hid_scales = [keep.tile([P, CH], U8, name="hs%d" % c, align_bytes=64) for c in range(NCH)]
+        y_rows = [keep.tile([P, PACK, CH], F32, name="yr%d" % c, align_bytes=64) for c in range(NCH)]
+        y_il = [keep.tile([P, CH, PACK], BF16, name="yi%d" % c, align_bytes=64) for c in range(NCH)]
+        out_rows = out_0.rearrange("(p t) j -> p t j", t=PACK)
+        out_words = out_1[0].rearrange("p n t -> p (n t)").bitcast(I32)
+
+        def first(c):
+            i, o = divmod(c * CH, HALF)
+            for t in range(PACK):
+                nc.tensor.matmul_mx(
+                    out=a_bank[c][:, t, :],
+                    lhsT=wa_d[:, t * P : (t + 1) * P].bitcast(FP8X4),
+                    lhsT_scale=was_d[:, t * P : (t + 1) * P],
+                    rhs=xg[i][:, o : o + CH].bitcast(FP4X4),
+                    rhs_scale=sg[i][:, o : o + CH],
+                    start=True,
+                    stop=True,
+                )
+
+        def relu(c):
+            nc.scalar.activation(out=h1[:, :, PAD + c * CH : PAD + (c + 1) * CH], in_=a_bank[c][:], func=ACT.Relu)
+
+        def mix(c):
+            lo = PAD + c * CH
+            for t in range(PACK):
+                nc.vector.scalar_tensor_tensor(
+                    out=hid_rows[c][:, t, :],
+                    in0=h1[:, t, lo - 1 : lo - 1 + CH],
+                    scalar=dc_sb[:, t : t + 1],
+                    in1=h1[:, t, lo : lo + CH],
+                    op0=ALU.mult,
+                    op1=ALU.add,
+                )
+
+        def weave(on_vector, dst, src):
+            d = dst[:].rearrange("p (c i) t -> p c t i", i=4)
+            s = src[:].rearrange("p t (c i) -> p c t i", i=4)
+            if on_vector:
+                nc.vector.tensor_copy(out=d, in_=s)
+            else:
+                nc.scalar.copy(out=d, in_=s)
+
+        def quant_hid(c):
+            nc.vector.quantize_mx(
+                out=hid_codes[c][:].bitcast(FP8X4),
+                scales=hid_scales[c][:],
+                in_=hid_il[c][:].rearrange("p j t -> p (j t)"),
+            )
+
+        def second(c):
+            for t in range(PACK):
+                nc.tensor.matmul_mx(
+                    out=p_bank[c][:, t, :],
+                    lhsT=wb_d[:, t * P : (t + 1) * P].bitcast(FP4X4),
+                    lhsT_scale=wbs_d[:, t * P : (t + 1) * P],
+                    rhs=hid_codes[c][:].bitcast(FP8X4),
+                    rhs_scale=hid_scales[c][:],
+                    start=True,
+                    stop=True,
+                )
+
+        def weigh(c):
+            cols = slice(c * CH, (c + 1) * CH)
+            nc.vector.tensor_tensor(
+                out=y_rows[c][:],
+                in0=p_bank[c][:],
+                in1=rw_sb[:, cols].unsqueeze(1).to_broadcast([P, PACK, CH]),
+                op=ALU.mult,
+            )
+            nc.sync.dma_start(out=out_rows[:, :, cols], in_=y_rows[c][:])
+
+        def quant_y(c):
+            cols = slice(c * CH, (c + 1) * CH)
+            nc.vector.quantize_mx(
+                out=y_codes[:, cols].bitcast(FP8X4),
+                scales=y_scales[:, cols],
+                in_=y_il[c][:].rearrange("p j t -> p (j t)"),
+            )
+
+        gather(0)
+        deal(wa_d, wa_raw)
+        deal(was_d, was_raw)
+        first(0)
+        first(1)
+        gather(1)
+        first(2)
+        first(3)
+        deal(wb_d, wb_raw)
+        deal(wbs_d, wbs_raw)
+        relu(0)
+        relu(1)
+        mix(0)
+        weave(True, hid_il[0], hid_rows[0])
+        mix(1)
+        quant_hid(0)
+        second(0)
+        relu(2)
+        weave(False, hid_il[1], hid_rows[1])
+        relu(3)
+        mix(2)
+        quant_hid(1)
+        second(1)
+        weave(False, hid_il[2], hid_rows[2])
+        mix(3)
+        weave(False, hid_il[3], hid_rows[3])
+        weigh(0)
+        quant_hid(2)
+        second(2)
+        weigh(1)
+        quant_hid(3)
+        second(3)
+        weave(False, y_il[0], y_rows[0])
+        weave(False, y_il[1], y_rows[1])
+        weigh(2)
+        quant_y(0)
+        weave(False, y_il[2], y_rows[2])
+        weigh(3)
+        quant_y(1)
+        nc.sync.dma_start(out=out_words[:, 0:HALF], in_=y_codes[:, 0:HALF].bitcast(I32))
+        weave(True, y_il[3], y_rows[3])
+        quant_y(2)
+        quant_y(3)
+        nc.sync.dma_start(out=out_words[:, HALF:J], in_=y_codes[:, HALF:J].bitcast(I32))
+        for q in range(4):
+            queue = nc.sync if q % 2 else nc.scalar
+            queue.dma_start(
+                out=out_2[0, 4 * q : 4 * q + 4, :].bitcast(I32), in_=y_scales[32 * q : 32 * q + 4, :].bitcast(I32)
+            )

@@ -1,6 +1,7 @@
 from contextlib import ExitStack
 
 import concourse.mybir as mybir
+from concourse.masks import make_identity
 
 F32 = mybir.dt.float32
 BF16 = mybir.dt.bfloat16
@@ -45,11 +46,12 @@ def tile_list_hidden_with_previous_pl_kernel(
         wb_d = keep.tile([P, W], U16, name="wb_d", align_bytes=64)
         wbs_d = keep.tile([P, W], U8, name="wbs_d", align_bytes=64)
         dc_sb = keep.tile([P, PACK], F32, name="dc_sb")
+        rw_col = keep.tile([P, PACK], F32, name="rw_col")
+        ident = keep.tile([P, P], F32, name="ident", align_bytes=64)
         rw_sb = keep.tile([P, J], F32, name="rw_sb")
         xg = [keep.tile([P, HALF], U16, name="xg%d" % i, align_bytes=64) for i in range(2)]
-        sg = [keep.tile([P, HALF], U8, name="sg%d" % i, align_bytes=64) for i in range(2)]
+        sg = keep.tile([P, J], U8, name="sg", align_bytes=64)
         h1 = keep.tile([P, PACK, J + 2 * PAD], F32, name="h1", align_bytes=64)
-        warm = keep.tile([P, 1], F32, name="warm")
         y_codes = keep.tile([P, J], U32, name="y_codes", align_bytes=64)
         y_scales = keep.tile([P, J], U8, name="y_scales", align_bytes=64)
 
@@ -64,27 +66,27 @@ def tile_list_hidden_with_previous_pl_kernel(
             )
 
         nc.vector.memset(xs_win[:].bitcast(I32), 0)
+        nc.vector.memset(ident[:], 0.0)
+        make_identity(nc, ident[:], nomemset=True)
+        nc.vector.memset(h1[:, :, 0:PAD], 0.0)
         nc.vector.memset(was_raw[:].bitcast(I32), 0)
         nc.vector.memset(wbs_raw[:].bitcast(I32), 0)
-        nc.vector.memset(h1[:, :, 0:PAD], 0.0)
 
         nc.sync.dma_start(offsets[:], offs)
+        nc.sync.dma_start(out=dc_sb[:], in_=dc.rearrange("(p t) o -> p (t o)", t=PACK))
+        nc.sync.dma_start(out=rw_col[:], in_=rw[0].rearrange("(p c) -> p c", c=PACK))
+        nc.sync.dma_start(out=xt_win[:].bitcast(I32), in_=xt_words[0].bitcast(I32))
         for q in range(4):
             load_scale_rows(nc.scalar, xs_win, xt_scales, q)
-        nc.sync.dma_start(out=xt_win[:].bitcast(I32), in_=xt_words[0].bitcast(I32))
         nc.sync.dma_start(out=wa_raw[:], in_=wa_words[0].rearrange("p n t -> p (n t)").bitcast(I32))
         for q in range(4):
             load_scale_rows(nc.sync, was_raw, wa_scales, q)
-        nc.gpsimd.dma_start(out=dc_sb[:], in_=dc.rearrange("(p t) o -> p (t o)", t=PACK))
         nc.sync.dma_start(out=wb_raw[:].bitcast(I32), in_=wb_words[0].bitcast(I32))
         for q in range(4):
             load_scale_rows(nc.sync, wbs_raw, wb_scales, q)
-        nc.gpsimd.dma_start(out=rw_sb[:], in_=rw[0].partition_broadcast(P))
-        nc.scalar.activation(out=warm[:], in_=h1[:, 0, 0:1], func=ACT.Relu)
 
         def gather(i):
             lst = offsets[:, i * (HALF // 16) : (i + 1) * (HALF // 16)]
-            nc.vector.tensor_copy(sg[i][:], xs_win[:].indirect(lst))
             nc.vector.tensor_copy(xg[i][:], xt_win[:].indirect(lst))
 
         a_bank = [psum.tile([P, PACK, CH], F32, name="a%d" % c) for c in range(NCH)]
@@ -106,7 +108,7 @@ def tile_list_hidden_with_previous_pl_kernel(
                     lhsT=wa_d[:, t * P : (t + 1) * P].bitcast(FP8X4),
                     lhsT_scale=was_d[:, t * P : (t + 1) * P],
                     rhs=xg[i][:, o : o + CH].bitcast(FP4X4),
-                    rhs_scale=sg[i][:, o : o + CH],
+                    rhs_scale=sg[:, c * CH : (c + 1) * CH],
                     start=True,
                     stop=True,
                 )
@@ -171,6 +173,15 @@ def tile_list_hidden_with_previous_pl_kernel(
                 in_=y_il[c][:].rearrange("p j t -> p (j t)"),
             )
 
+        def spread_rw():
+            for c in range(PACK):
+                nc.tensor.transpose(p_bank[NCH - 1][:, c, :], rw_col[:, c : c + 1].to_broadcast([P, P]), ident[:])
+            nc.scalar.copy(
+                out=rw_sb[:].rearrange("p (n c) -> p n c", c=PACK), in_=p_bank[NCH - 1][:].rearrange("p c n -> p n c")
+            )
+
+        spread_rw()
+        nc.vector.tensor_copy(sg[:], xs_win[:].indirect(offsets[:]))
         gather(0)
         deal(wa_d, wa_raw)
         deal(was_d, was_raw)

@@ -1,7 +1,6 @@
 from contextlib import ExitStack
 
 import concourse.mybir as mybir
-from concourse.masks import make_identity
 
 F32 = mybir.dt.float32
 BF16 = mybir.dt.bfloat16
@@ -15,15 +14,18 @@ ALU = mybir.AluOpType
 ACT = mybir.ActivationFunctionType
 
 P = 128
-T = 2048
-J = 512
-W = 512
 PACK = 4
-CH = 128
-NCH = J // CH
-HALF = 256
+QUADRANTS = 4
+TOKENS = 2048
+SLOTS = 512
+FEATURES = 512
+CHUNK = 128
+CHUNKS = SLOTS // CHUNK
+HALF = SLOTS // 2
+GROUP = 16
 PAD = 4
-FLOPS = 2 * 2 * 512 * 512 * 512
+RUN = 4
+FLOPS = 2 * 2 * FEATURES * FEATURES * SLOTS
 
 
 def tile_list_hidden_with_previous_pl_kernel(
@@ -32,202 +34,192 @@ def tile_list_hidden_with_previous_pl_kernel(
     nc = tc.nc
     with ExitStack() as ctx:
         keep = ctx.enter_context(tc.tile_pool(name="keep", bufs=1))
+        shared = ctx.enter_context(tc.tile_pool(name="shared", bufs=1))
         psum = ctx.enter_context(tc.psum_pool(name="psum", bufs=1))
 
-        offsets = keep.tile([P, J // 16], U16, name="offsets")
-        xt_win = keep.tile([P, T], U16, name="xt_win", align_bytes=64)
-        xs_win = keep.tile([P, T], U8, name="xs_win", align_bytes=64)
-        wa_raw = keep.tile([P, W], I32, name="wa_raw", align_bytes=64)
-        was_raw = keep.tile([P, W], U8, name="was_raw", align_bytes=64)
-        wb_raw = keep.tile([P, W], U16, name="wb_raw", align_bytes=64)
-        wbs_raw = keep.tile([P, W], U8, name="wbs_raw", align_bytes=64)
-        wa_d = keep.tile([P, W], I32, name="wa_d", align_bytes=64)
-        was_d = keep.tile([P, W], U8, name="was_d", align_bytes=64)
-        wb_d = keep.tile([P, W], U16, name="wb_d", align_bytes=64)
-        wbs_d = keep.tile([P, W], U8, name="wbs_d", align_bytes=64)
-        dc_sb = keep.tile([P, PACK], F32, name="dc_sb")
-        rw_col = keep.tile([P, PACK], F32, name="rw_col")
-        ident = keep.tile([P, P], F32, name="ident", align_bytes=64)
-        rw_sb = keep.tile([P, J], F32, name="rw_sb")
-        xg = [keep.tile([P, HALF], U16, name="xg%d" % i, align_bytes=64) for i in range(2)]
-        sg = keep.tile([P, J], U8, name="sg", align_bytes=64)
-        h1 = keep.tile([P, PACK, J + 2 * PAD], F32, name="h1", align_bytes=64)
-        y_codes = keep.tile([P, J], U32, name="y_codes", align_bytes=64)
-        y_scales = keep.tile([P, J], U8, name="y_scales", align_bytes=64)
-
-        def load_scale_rows(queue, tile, src, q):
-            queue.dma_start(
-                out=tile[32 * q : 32 * q + 4, :].bitcast(I32), in_=src[0, 4 * q : 4 * q + 4, :].bitcast(I32)
-            )
-
-        def deal(dst, src):
-            nc.vector.tensor_copy(
-                out=dst[:].rearrange("p (t q) -> p t q", t=PACK), in_=src[:].rearrange("p (q t) -> p t q", t=PACK)
-            )
-
-        nc.vector.memset(xs_win[:].bitcast(I32), 0)
-        nc.vector.memset(ident[:], 0.0)
-        make_identity(nc, ident[:], nomemset=True)
-        nc.vector.memset(h1[:, :, 0:PAD], 0.0)
-        nc.vector.memset(was_raw[:].bitcast(I32), 0)
-        nc.vector.memset(wbs_raw[:].bitcast(I32), 0)
-
-        nc.sync.dma_start(offsets[:], offs)
-        nc.sync.dma_start(out=dc_sb[:], in_=dc.rearrange("(p t) o -> p (t o)", t=PACK))
-        nc.sync.dma_start(out=rw_col[:], in_=rw[0].rearrange("(p c) -> p c", c=PACK))
-        nc.sync.dma_start(out=xt_win[:].bitcast(I32), in_=xt_words[0].bitcast(I32))
-        for q in range(4):
-            load_scale_rows(nc.scalar, xs_win, xt_scales, q)
-        nc.sync.dma_start(out=wa_raw[:], in_=wa_words[0].rearrange("p n t -> p (n t)").bitcast(I32))
-        for q in range(4):
-            load_scale_rows(nc.sync, was_raw, wa_scales, q)
-        nc.sync.dma_start(out=wb_raw[:].bitcast(I32), in_=wb_words[0].bitcast(I32))
-        for q in range(4):
-            load_scale_rows(nc.sync, wbs_raw, wb_scales, q)
-
-        def gather(i):
-            lst = offsets[:, i * (HALF // 16) : (i + 1) * (HALF // 16)]
-            nc.vector.tensor_copy(xg[i][:], xt_win[:].indirect(lst))
-
-        a_bank = [psum.tile([P, PACK, CH], F32, name="a%d" % c) for c in range(NCH)]
-        p_bank = [psum.tile([P, PACK, CH], F32, name="p%d" % c) for c in range(NCH)]
-        hid_rows = [keep.tile([P, PACK, CH], BF16, name="hr%d" % c, align_bytes=64) for c in range(NCH)]
-        hid_il = [keep.tile([P, CH, PACK], BF16, name="hi%d" % c, align_bytes=64) for c in range(NCH)]
-        hid_codes = [keep.tile([P, CH], U32, name="hc%d" % c, align_bytes=64) for c in range(NCH)]
-        hid_scales = [keep.tile([P, CH], U8, name="hs%d" % c, align_bytes=64) for c in range(NCH)]
-        y_rows = [keep.tile([P, PACK, CH], F32, name="yr%d" % c, align_bytes=64) for c in range(NCH)]
-        y_il = [keep.tile([P, CH, PACK], BF16, name="yi%d" % c, align_bytes=64) for c in range(NCH)]
+        offsets = keep.tile([P, SLOTS // GROUP], U16, name="offsets")
+        xt_window = keep.tile([P, TOKENS], U16, name="xt_window", align_bytes=64)
+        xt_scale_window = keep.tile([P, TOKENS], U8, name="xt_scale_window", align_bytes=64)
+        wa_loaded = shared.tile([P, FEATURES], I32, name="wa_loaded", align_bytes=64, offset=0)
+        wa_scale_loaded = keep.tile([P, FEATURES], U8, name="wa_scale_loaded", align_bytes=64)
+        wb_loaded = keep.tile([P, FEATURES], U16, name="wb_loaded", align_bytes=64)
+        wb_scale_loaded = keep.tile([P, FEATURES], U8, name="wb_scale_loaded", align_bytes=64)
+        wa_dealt = keep.tile([P, FEATURES], I32, name="wa_dealt", align_bytes=64)
+        wa_scale_dealt = keep.tile([P, FEATURES], U8, name="wa_scale_dealt", align_bytes=64)
+        wb_dealt = keep.tile([P, FEATURES], U16, name="wb_dealt", align_bytes=64)
+        wb_scale_dealt = keep.tile([P, FEATURES], U8, name="wb_scale_dealt", align_bytes=64)
+        dc_dealt = keep.tile([P, PACK], F32, name="dc_dealt")
+        rw_spread = keep.tile([P, SLOTS], F32, name="rw_spread")
+        picked = [
+            keep.tile([P, HALF], U16, name="picked0", align_bytes=64),
+            shared.tile([P, HALF], U16, name="picked1", align_bytes=64, offset=0),
+        ]
+        picked_scale = [
+            keep.tile([P, HALF], U8, name="picked_scale0", align_bytes=64),
+            shared.tile([P, HALF], U8, name="picked_scale1", align_bytes=64, offset=2 * HALF),
+        ]
+        h1 = keep.tile([P, PACK, SLOTS + 2 * PAD], F32, name="h1", align_bytes=64)
+        y_codes = keep.tile([P, SLOTS], U32, name="y_codes", align_bytes=64)
+        y_scales = keep.tile([P, SLOTS], U8, name="y_scales", align_bytes=64)
+        a_bank = [psum.tile([P, PACK, CHUNK], F32, name="a_bank%d" % c) for c in range(CHUNKS)]
+        p_bank = [psum.tile([P, PACK, CHUNK], F32, name="p_bank%d" % c) for c in range(CHUNKS)]
+        hid_rows = [keep.tile([P, PACK, CHUNK], BF16, name="hid_rows%d" % c, align_bytes=64) for c in range(CHUNKS)]
+        hid_woven = [keep.tile([P, CHUNK, PACK], BF16, name="hid_woven%d" % c, align_bytes=64) for c in range(CHUNKS)]
+        hid_codes = [keep.tile([P, CHUNK], U32, name="hid_codes%d" % c, align_bytes=64) for c in range(CHUNKS)]
+        hid_scales = [keep.tile([P, CHUNK], U8, name="hid_scales%d" % c, align_bytes=64) for c in range(CHUNKS)]
+        y_rows = [keep.tile([P, PACK, CHUNK], F32, name="y_rows%d" % c, align_bytes=64) for c in range(CHUNKS)]
+        y_woven = [keep.tile([P, CHUNK, PACK], BF16, name="y_woven%d" % c, align_bytes=64) for c in range(CHUNKS)]
         out_rows = out_0.rearrange("(p t) j -> p t j", t=PACK)
-        out_words = out_1[0].rearrange("p n t -> p (n t)").bitcast(I32)
+        out_words = out_1[0].rearrange("p j t -> p (j t)").bitcast(I32)
 
-        def first(c):
-            i, o = divmod(c * CH, HALF)
+        def scale_rows(tile, quadrant):
+            return tile[32 * quadrant : 32 * quadrant + 4, :].bitcast(I32)
+
+        def hbm_scale_rows(scales, quadrant):
+            return scales[0, 4 * quadrant : 4 * quadrant + 4, :].bitcast(I32)
+
+        def either_queue(quadrant):
+            return nc.scalar if quadrant % 2 else nc.sync
+
+        def deal(dealt, loaded):
+            nc.vector.tensor_copy(
+                out=dealt[:].rearrange("p (t q) -> p t q", t=PACK), in_=loaded[:].rearrange("p (q t) -> p t q", t=PACK)
+            )
+
+        def gather(half):
+            entries = offsets[:, half * (HALF // GROUP) : (half + 1) * (HALF // GROUP)]
+            nc.vector.tensor_copy(picked[half][:], xt_window[:].indirect(entries))
+            nc.vector.tensor_copy(picked_scale[half][:], xt_scale_window[:].indirect(entries))
+
+        def first_layer(c):
+            half, start = divmod(c * CHUNK, HALF)
             for t in range(PACK):
                 nc.tensor.matmul_mx(
                     out=a_bank[c][:, t, :],
-                    lhsT=wa_d[:, t * P : (t + 1) * P].bitcast(FP8X4),
-                    lhsT_scale=was_d[:, t * P : (t + 1) * P],
-                    rhs=xg[i][:, o : o + CH].bitcast(FP4X4),
-                    rhs_scale=sg[:, c * CH : (c + 1) * CH],
+                    lhsT=wa_dealt[:, t * P : (t + 1) * P].bitcast(FP8X4),
+                    lhsT_scale=wa_scale_dealt[:, t * P : (t + 1) * P],
+                    rhs=picked[half][:, start : start + CHUNK].bitcast(FP4X4),
+                    rhs_scale=picked_scale[half][:, start : start + CHUNK],
                     start=True,
                     stop=True,
                 )
 
         def relu(c):
-            nc.scalar.activation(out=h1[:, :, PAD + c * CH : PAD + (c + 1) * CH], in_=a_bank[c][:], func=ACT.Relu)
+            nc.scalar.activation(out=h1[:, :, PAD + c * CHUNK : PAD + (c + 1) * CHUNK], in_=a_bank[c][:], func=ACT.Relu)
 
-        def mix(c):
-            lo = PAD + c * CH
+        def add_previous(c):
+            first = PAD + c * CHUNK
             for t in range(PACK):
                 nc.vector.scalar_tensor_tensor(
                     out=hid_rows[c][:, t, :],
-                    in0=h1[:, t, lo - 1 : lo - 1 + CH],
-                    scalar=dc_sb[:, t : t + 1],
-                    in1=h1[:, t, lo : lo + CH],
+                    in0=h1[:, t, first - 1 : first - 1 + CHUNK],
+                    scalar=dc_dealt[:, t : t + 1],
+                    in1=h1[:, t, first : first + CHUNK],
                     op0=ALU.mult,
                     op1=ALU.add,
                 )
 
-        def weave(on_vector, dst, src):
-            d = dst[:].rearrange("p (c i) t -> p c t i", i=4)
-            s = src[:].rearrange("p t (c i) -> p c t i", i=4)
-            if on_vector:
-                nc.vector.tensor_copy(out=d, in_=s)
-            else:
-                nc.scalar.copy(out=d, in_=s)
+        def weave(copy, woven, rows):
+            copy(
+                out=woven[:].rearrange("p (c i) t -> p c t i", i=RUN),
+                in_=rows[:].rearrange("p t (c i) -> p c t i", i=RUN),
+            )
 
-        def quant_hid(c):
+        def second_layer(c):
             nc.vector.quantize_mx(
                 out=hid_codes[c][:].bitcast(FP8X4),
                 scales=hid_scales[c][:],
-                in_=hid_il[c][:].rearrange("p j t -> p (j t)"),
+                in_=hid_woven[c][:].rearrange("p j t -> p (j t)"),
             )
-
-        def second(c):
             for t in range(PACK):
                 nc.tensor.matmul_mx(
                     out=p_bank[c][:, t, :],
-                    lhsT=wb_d[:, t * P : (t + 1) * P].bitcast(FP4X4),
-                    lhsT_scale=wbs_d[:, t * P : (t + 1) * P],
+                    lhsT=wb_dealt[:, t * P : (t + 1) * P].bitcast(FP4X4),
+                    lhsT_scale=wb_scale_dealt[:, t * P : (t + 1) * P],
                     rhs=hid_codes[c][:].bitcast(FP8X4),
                     rhs_scale=hid_scales[c][:],
                     start=True,
                     stop=True,
                 )
 
-        def weigh(c):
-            cols = slice(c * CH, (c + 1) * CH)
+        def weigh_and_store(c):
+            slots = slice(c * CHUNK, (c + 1) * CHUNK)
             nc.vector.tensor_tensor(
                 out=y_rows[c][:],
                 in0=p_bank[c][:],
-                in1=rw_sb[:, cols].unsqueeze(1).to_broadcast([P, PACK, CH]),
+                in1=rw_spread[:, slots].unsqueeze(1).to_broadcast([P, PACK, CHUNK]),
                 op=ALU.mult,
             )
-            nc.sync.dma_start(out=out_rows[:, :, cols], in_=y_rows[c][:])
+            nc.sync.dma_start(out=out_rows[:, :, slots], in_=y_rows[c][:])
 
-        def quant_y(c):
-            cols = slice(c * CH, (c + 1) * CH)
+        def quantize_y(c):
+            slots = slice(c * CHUNK, (c + 1) * CHUNK)
             nc.vector.quantize_mx(
-                out=y_codes[:, cols].bitcast(FP8X4),
-                scales=y_scales[:, cols],
-                in_=y_il[c][:].rearrange("p j t -> p (j t)"),
+                out=y_codes[:, slots].bitcast(FP8X4),
+                scales=y_scales[:, slots],
+                in_=y_woven[c][:].rearrange("p j t -> p (j t)"),
             )
 
-        def spread_rw():
-            for c in range(PACK):
-                nc.tensor.transpose(p_bank[NCH - 1][:, c, :], rw_col[:, c : c + 1].to_broadcast([P, P]), ident[:])
-            nc.scalar.copy(
-                out=rw_sb[:].rearrange("p (n c) -> p n c", c=PACK), in_=p_bank[NCH - 1][:].rearrange("p c n -> p n c")
-            )
+        nc.vector.memset(wa_scale_loaded[:].bitcast(I32), 0)
+        nc.vector.memset(xt_scale_window[:].bitcast(I32), 0)
+        nc.vector.memset(wb_scale_loaded[:].bitcast(I32), 0)
+        nc.vector.memset(h1[:, :, PAD - 1 : PAD], 0.0)
 
-        spread_rw()
-        nc.vector.tensor_copy(sg[:], xs_win[:].indirect(offsets[:]))
+        nc.gpsimd.dma_start(out=dc_dealt[:], in_=dc.rearrange("(p t) o -> p (t o)", t=PACK))
+        nc.sync.dma_start(offsets[:], offs)
+        for quadrant in range(QUADRANTS):
+            either_queue(quadrant).dma_start(
+                out=scale_rows(wa_scale_loaded, quadrant), in_=hbm_scale_rows(wa_scales, quadrant)
+            )
+        nc.sync.dma_start(out=xt_window[:].bitcast(I32), in_=xt_words[0].bitcast(I32))
+        for quadrant in range(QUADRANTS):
+            nc.sync.dma_start(out=scale_rows(xt_scale_window, quadrant), in_=hbm_scale_rows(xt_scales, quadrant))
+        nc.sync.dma_start(out=wa_loaded[:], in_=wa_words[0].rearrange("p n t -> p (n t)").bitcast(I32))
+        nc.sync.dma_start(out=wb_loaded[:].bitcast(I32), in_=wb_words[0].bitcast(I32))
+        for quadrant in range(QUADRANTS):
+            nc.sync.dma_start(out=scale_rows(wb_scale_loaded, quadrant), in_=hbm_scale_rows(wb_scales, quadrant))
+        nc.sync.dma_start(out=rw_spread[:], in_=rw[0].partition_broadcast(P))
+
+        deal(wa_scale_dealt, wa_scale_loaded)
         gather(0)
-        deal(wa_d, wa_raw)
-        deal(was_d, was_raw)
-        first(0)
-        first(1)
+        deal(wa_dealt, wa_loaded)
+        first_layer(0)
+        first_layer(1)
         gather(1)
-        first(2)
-        first(3)
-        deal(wb_d, wb_raw)
-        deal(wbs_d, wbs_raw)
+        first_layer(2)
+        first_layer(3)
+        deal(wb_dealt, wb_loaded)
+        deal(wb_scale_dealt, wb_scale_loaded)
+
         relu(0)
         relu(1)
-        mix(0)
-        weave(True, hid_il[0], hid_rows[0])
-        mix(1)
-        quant_hid(0)
-        second(0)
+        add_previous(0)
+        add_previous(1)
+        weave(nc.vector.tensor_copy, hid_woven[0], hid_rows[0])
         relu(2)
-        weave(False, hid_il[1], hid_rows[1])
+        weave(nc.scalar.copy, hid_woven[1], hid_rows[1])
         relu(3)
-        mix(2)
-        quant_hid(1)
-        second(1)
-        weave(False, hid_il[2], hid_rows[2])
-        mix(3)
-        weave(False, hid_il[3], hid_rows[3])
-        weigh(0)
-        quant_hid(2)
-        second(2)
-        weigh(1)
-        quant_hid(3)
-        second(3)
-        weave(False, y_il[0], y_rows[0])
-        weave(False, y_il[1], y_rows[1])
-        weigh(2)
-        quant_y(0)
-        weave(False, y_il[2], y_rows[2])
-        weigh(3)
-        quant_y(1)
+        add_previous(2)
+        second_layer(0)
+        weave(nc.scalar.copy, hid_woven[2], hid_rows[2])
+        add_previous(3)
+        second_layer(1)
+        weave(nc.scalar.copy, hid_woven[3], hid_rows[3])
+        weigh_and_store(0)
+        second_layer(2)
+        weigh_and_store(1)
+        second_layer(3)
+        weave(nc.scalar.copy, y_woven[0], y_rows[0])
+        weave(nc.scalar.copy, y_woven[1], y_rows[1])
+        weigh_and_store(2)
+        quantize_y(0)
+        weave(nc.scalar.copy, y_woven[2], y_rows[2])
+        weigh_and_store(3)
+        quantize_y(1)
         nc.sync.dma_start(out=out_words[:, 0:HALF], in_=y_codes[:, 0:HALF].bitcast(I32))
-        weave(True, y_il[3], y_rows[3])
-        quant_y(2)
-        quant_y(3)
-        nc.sync.dma_start(out=out_words[:, HALF:J], in_=y_codes[:, HALF:J].bitcast(I32))
-        for q in range(4):
-            queue = nc.sync if q % 2 else nc.scalar
-            queue.dma_start(
-                out=out_2[0, 4 * q : 4 * q + 4, :].bitcast(I32), in_=y_scales[32 * q : 32 * q + 4, :].bitcast(I32)
-            )
+        weave(nc.vector.tensor_copy, y_woven[3], y_rows[3])
+        quantize_y(2)
+        quantize_y(3)
+        nc.scalar.dma_start(out=out_words[:, HALF:SLOTS], in_=y_codes[:, HALF:SLOTS].bitcast(I32))
+        for quadrant in range(QUADRANTS):
+            either_queue(quadrant).dma_start(out=hbm_scale_rows(out_2, quadrant), in_=scale_rows(y_scales, quadrant))

from contextlib import ExitStack

import concourse.mybir as mybir

F32 = mybir.dt.float32
BF16 = mybir.dt.bfloat16
I32 = mybir.dt.int32
U32 = mybir.dt.uint32
U16 = mybir.dt.uint16
U8 = mybir.dt.uint8
FP8X4 = mybir.dt.float8_e4m3fn_x4
FP4X4 = mybir.dt.float4_e2m1fn_x4
ALU = mybir.AluOpType
ACT = mybir.ActivationFunctionType

P = 128
PACK = 4
QUADRANTS = 4
TOKENS = 2048
SLOTS = 512
FEATURES = 512
CHUNK = 128
CHUNKS = SLOTS // CHUNK
HALF = SLOTS // 2
GROUP = 16
PAD = 4
RUN = 4
FLOPS = 2 * 2 * FEATURES * FEATURES * SLOTS


def tile_list_hidden_with_previous_pl_kernel(
    tc, xt_words, xt_scales, wa_words, wa_scales, dc, wb_words, wb_scales, rw, offs, out_0, out_1, out_2
):
    nc = tc.nc
    with ExitStack() as ctx:
        keep = ctx.enter_context(tc.tile_pool(name="keep", bufs=1))
        shared = ctx.enter_context(tc.tile_pool(name="shared", bufs=1))
        psum = ctx.enter_context(tc.psum_pool(name="psum", bufs=1))

        offsets = keep.tile([P, SLOTS // GROUP], U16, name="offsets")
        xt_window = keep.tile([P, TOKENS], U16, name="xt_window", align_bytes=64)
        xt_scale_window = keep.tile([P, TOKENS], U8, name="xt_scale_window", align_bytes=64)
        wa_loaded = shared.tile([P, FEATURES], I32, name="wa_loaded", align_bytes=64, offset=0)
        wa_scale_loaded = keep.tile([P, FEATURES], U8, name="wa_scale_loaded", align_bytes=64)
        wb_loaded = keep.tile([P, FEATURES], U16, name="wb_loaded", align_bytes=64)
        wb_scale_loaded = keep.tile([P, FEATURES], U8, name="wb_scale_loaded", align_bytes=64)
        wa_dealt = keep.tile([P, FEATURES], I32, name="wa_dealt", align_bytes=64)
        wa_scale_dealt = keep.tile([P, FEATURES], U8, name="wa_scale_dealt", align_bytes=64)
        wb_dealt = keep.tile([P, FEATURES], U16, name="wb_dealt", align_bytes=64)
        wb_scale_dealt = keep.tile([P, FEATURES], U8, name="wb_scale_dealt", align_bytes=64)
        dc_dealt = keep.tile([P, PACK], F32, name="dc_dealt")
        rw_spread = keep.tile([P, SLOTS], F32, name="rw_spread")
        picked = [
            keep.tile([P, HALF], U16, name="picked0", align_bytes=64),
            shared.tile([P, HALF], U16, name="picked1", align_bytes=64, offset=0),
        ]
        picked_scale = [
            keep.tile([P, HALF], U8, name="picked_scale0", align_bytes=64),
            shared.tile([P, HALF], U8, name="picked_scale1", align_bytes=64, offset=2 * HALF),
        ]
        h1 = keep.tile([P, PACK, SLOTS + 2 * PAD], F32, name="h1", align_bytes=64)
        y_codes = keep.tile([P, SLOTS], U32, name="y_codes", align_bytes=64)
        y_scales = keep.tile([P, SLOTS], U8, name="y_scales", align_bytes=64)
        a_bank = [psum.tile([P, PACK, CHUNK], F32, name="a_bank%d" % c) for c in range(CHUNKS)]
        p_bank = [psum.tile([P, PACK, CHUNK], F32, name="p_bank%d" % c) for c in range(CHUNKS)]
        hid_rows = [keep.tile([P, PACK, CHUNK], BF16, name="hid_rows%d" % c, align_bytes=64) for c in range(CHUNKS)]
        hid_woven = [keep.tile([P, CHUNK, PACK], BF16, name="hid_woven%d" % c, align_bytes=64) for c in range(CHUNKS)]
        hid_codes = [keep.tile([P, CHUNK], U32, name="hid_codes%d" % c, align_bytes=64) for c in range(CHUNKS)]
        hid_scales = [keep.tile([P, CHUNK], U8, name="hid_scales%d" % c, align_bytes=64) for c in range(CHUNKS)]
        y_rows = [keep.tile([P, PACK, CHUNK], F32, name="y_rows%d" % c, align_bytes=64) for c in range(CHUNKS)]
        y_woven = [keep.tile([P, CHUNK, PACK], BF16, name="y_woven%d" % c, align_bytes=64) for c in range(CHUNKS)]
        out_rows = out_0.rearrange("(p t) j -> p t j", t=PACK)
        out_words = out_1[0].rearrange("p j t -> p (j t)").bitcast(I32)

        def scale_rows(tile, quadrant):
            return tile[32 * quadrant : 32 * quadrant + 4, :].bitcast(I32)

        def hbm_scale_rows(scales, quadrant):
            return scales[0, 4 * quadrant : 4 * quadrant + 4, :].bitcast(I32)

        def either_queue(quadrant):
            return nc.scalar if quadrant % 2 else nc.sync

        def deal(dealt, loaded):
            nc.vector.tensor_copy(
                out=dealt[:].rearrange("p (t q) -> p t q", t=PACK), in_=loaded[:].rearrange("p (q t) -> p t q", t=PACK)
            )

        def gather(half):
            entries = offsets[:, half * (HALF // GROUP) : (half + 1) * (HALF // GROUP)]
            nc.vector.tensor_copy(picked[half][:], xt_window[:].indirect(entries))
            nc.vector.tensor_copy(picked_scale[half][:], xt_scale_window[:].indirect(entries))

        def first_layer(c):
            half, start = divmod(c * CHUNK, HALF)
            for t in range(PACK):
                nc.tensor.matmul_mx(
                    out=a_bank[c][:, t, :],
                    lhsT=wa_dealt[:, t * P : (t + 1) * P].bitcast(FP8X4),
                    lhsT_scale=wa_scale_dealt[:, t * P : (t + 1) * P],
                    rhs=picked[half][:, start : start + CHUNK].bitcast(FP4X4),
                    rhs_scale=picked_scale[half][:, start : start + CHUNK],
                    start=True,
                    stop=True,
                )

        def relu(c):
            nc.scalar.activation(out=h1[:, :, PAD + c * CHUNK : PAD + (c + 1) * CHUNK], in_=a_bank[c][:], func=ACT.Relu)

        def add_previous(c):
            first = PAD + c * CHUNK
            for t in range(PACK):
                nc.vector.scalar_tensor_tensor(
                    out=hid_rows[c][:, t, :],
                    in0=h1[:, t, first - 1 : first - 1 + CHUNK],
                    scalar=dc_dealt[:, t : t + 1],
                    in1=h1[:, t, first : first + CHUNK],
                    op0=ALU.mult,
                    op1=ALU.add,
                )

        def weave(copy, woven, rows):
            copy(
                out=woven[:].rearrange("p (c i) t -> p c t i", i=RUN),
                in_=rows[:].rearrange("p t (c i) -> p c t i", i=RUN),
            )

        def second_layer(c):
            nc.vector.quantize_mx(
                out=hid_codes[c][:].bitcast(FP8X4),
                scales=hid_scales[c][:],
                in_=hid_woven[c][:].rearrange("p j t -> p (j t)"),
            )
            for t in range(PACK):
                nc.tensor.matmul_mx(
                    out=p_bank[c][:, t, :],
                    lhsT=wb_dealt[:, t * P : (t + 1) * P].bitcast(FP4X4),
                    lhsT_scale=wb_scale_dealt[:, t * P : (t + 1) * P],
                    rhs=hid_codes[c][:].bitcast(FP8X4),
                    rhs_scale=hid_scales[c][:],
                    start=True,
                    stop=True,
                )

        def weigh_and_store(c):
            slots = slice(c * CHUNK, (c + 1) * CHUNK)
            nc.vector.tensor_tensor(
                out=y_rows[c][:],
                in0=p_bank[c][:],
                in1=rw_spread[:, slots].unsqueeze(1).to_broadcast([P, PACK, CHUNK]),
                op=ALU.mult,
            )
            nc.sync.dma_start(out=out_rows[:, :, slots], in_=y_rows[c][:])

        def quantize_y(c):
            slots = slice(c * CHUNK, (c + 1) * CHUNK)
            nc.vector.quantize_mx(
                out=y_codes[:, slots].bitcast(FP8X4),
                scales=y_scales[:, slots],
                in_=y_woven[c][:].rearrange("p j t -> p (j t)"),
            )

        nc.vector.memset(wa_scale_loaded[:].bitcast(I32), 0)
        nc.vector.memset(xt_scale_window[:].bitcast(I32), 0)
        nc.vector.memset(wb_scale_loaded[:].bitcast(I32), 0)
        nc.vector.memset(h1[:, :, PAD - 1 : PAD], 0.0)

        nc.gpsimd.dma_start(out=dc_dealt[:], in_=dc.rearrange("(p t) o -> p (t o)", t=PACK))
        nc.sync.dma_start(offsets[:], offs)
        for quadrant in range(QUADRANTS):
            either_queue(quadrant).dma_start(
                out=scale_rows(wa_scale_loaded, quadrant), in_=hbm_scale_rows(wa_scales, quadrant)
            )
        nc.sync.dma_start(out=xt_window[:].bitcast(I32), in_=xt_words[0].bitcast(I32))
        for quadrant in range(QUADRANTS):
            nc.sync.dma_start(out=scale_rows(xt_scale_window, quadrant), in_=hbm_scale_rows(xt_scales, quadrant))
        nc.sync.dma_start(out=wa_loaded[:], in_=wa_words[0].rearrange("p n t -> p (n t)").bitcast(I32))
        nc.sync.dma_start(out=wb_loaded[:].bitcast(I32), in_=wb_words[0].bitcast(I32))
        for quadrant in range(QUADRANTS):
            nc.sync.dma_start(out=scale_rows(wb_scale_loaded, quadrant), in_=hbm_scale_rows(wb_scales, quadrant))
        nc.sync.dma_start(out=rw_spread[:], in_=rw[0].partition_broadcast(P))

        deal(wa_scale_dealt, wa_scale_loaded)
        gather(0)
        deal(wa_dealt, wa_loaded)
        first_layer(0)
        first_layer(1)
        gather(1)
        first_layer(2)
        first_layer(3)
        deal(wb_dealt, wb_loaded)
        deal(wb_scale_dealt, wb_scale_loaded)

        relu(0)
        relu(1)
        add_previous(0)
        add_previous(1)
        weave(nc.vector.tensor_copy, hid_woven[0], hid_rows[0])
        relu(2)
        weave(nc.scalar.copy, hid_woven[1], hid_rows[1])
        relu(3)
        add_previous(2)
        second_layer(0)
        weave(nc.scalar.copy, hid_woven[2], hid_rows[2])
        add_previous(3)
        second_layer(1)
        weave(nc.scalar.copy, hid_woven[3], hid_rows[3])
        weigh_and_store(0)
        second_layer(2)
        weigh_and_store(1)
        second_layer(3)
        weave(nc.scalar.copy, y_woven[0], y_rows[0])
        weave(nc.scalar.copy, y_woven[1], y_rows[1])
        weigh_and_store(2)
        quantize_y(0)
        weave(nc.scalar.copy, y_woven[2], y_rows[2])
        weigh_and_store(3)
        quantize_y(1)
        nc.sync.dma_start(out=out_words[:, 0:HALF], in_=y_codes[:, 0:HALF].bitcast(I32))
        weave(nc.vector.tensor_copy, y_woven[3], y_rows[3])
        quantize_y(2)
        quantize_y(3)
        nc.scalar.dma_start(out=out_words[:, HALF:SLOTS], in_=y_codes[:, HALF:SLOTS].bitcast(I32))
        for quadrant in range(QUADRANTS):
            either_queue(quadrant).dma_start(out=hbm_scale_rows(out_2, quadrant), in_=scale_rows(y_scales, quadrant))
